import numpy as np
import ml_dtypes


def mxq(x, axis, fmt="e4m3"):
    dtype, down = {"e4m3": (ml_dtypes.float8_e4m3fn, 7), "e5m2": (ml_dtypes.float8_e5m2, 14)}[fmt]
    v = np.moveaxis(np.asarray(x, np.float32).astype(ml_dtypes.bfloat16).astype(np.float64), axis, -1)
    blocks = v.reshape(v.shape[:-1] + (-1, 32))
    amax = np.abs(blocks).max(-1, keepdims=True)
    byte = np.maximum(np.where(amax > 0, np.frexp(amax)[1] - 1 + 127, 0) - down, 1)
    scale = np.exp2(byte - 127.0)
    codes = (blocks / scale).astype(np.float32).astype(dtype).astype(np.float64)
    return np.moveaxis((codes * scale).reshape(v.shape), -1, axis)


WIDE = False


def mx_kscale(k):
    if not WIDE:
        return np.ones(k)
    levels = np.array([10, -10, 5, -5, 0])
    if k % 512:
        return np.exp2(np.random.permutation(np.resize(levels, k // 32))).repeat(32)
    a = np.empty((k // 512, 16))
    for p in range(k // 512):
        a[p, :8] = np.random.permutation(np.resize(levels, 8))
        for g in range(8):
            far = levels[np.abs(levels - a[p, g]) >= 10]
            a[p, g + 8] = far[np.random.randint(len(far))]
    return np.exp2(a.ravel()).repeat(32)


def f64(x):
    return np.asarray(x).astype(np.float64)


def striped(idx):
    return np.tile(idx.reshape(-1, 16).T, (8, 1)).astype(np.uint16)


def unstriped(offs):
    return offs[:16].T.reshape(-1).astype(np.int64)


def pack_weight(w):
    k, n = w.shape
    w = f64(np.asarray(w, np.float32).astype(ml_dtypes.bfloat16)).reshape(k // 32, 32, n)
    amax = np.abs(w).max(1)
    byte = np.clip(np.where(amax > 0, np.frexp(amax)[1] - 1 + 127 - 7, 1), 1, 254)
    scaled = (w * np.exp2(127.0 - byte)[:, None, :]).reshape(k, n).astype(np.float32)
    words = np.ascontiguousarray(scaled.reshape(k // 512, 128, 4, n).transpose(0, 1, 3, 2)).astype(ml_dtypes.float8_e4m3fn).view(np.uint8)
    return words, np.ascontiguousarray(byte.astype(np.uint8).reshape(k // 512, 16, n))


def unpack_weight(words, scales):
    g, p, n, _ = words.shape
    vals = np.ascontiguousarray(words).view(ml_dtypes.float8_e4m3fn).astype(np.float64) * np.repeat(np.exp2(scales.astype(np.float64) - 127.0), 8, axis=1)[..., None]
    return vals.transpose(0, 1, 3, 2).reshape(g * 512, n)


K, T, S, N, H, J, W = 512, 2048, 256, 512, 512, 512, 128


def setup_inputs():
    n = np.random.standard_normal
    s = mx_kscale(K)[:, None]
    u = mx_kscale(H)
    packed_xT = pack_weight(n((K, T)) * s)
    perm = np.random.permutation(S)
    return {
        "x_words": packed_xT[0],
        "x_scales": packed_xT[1],
        "w1": (n((K, H)) / np.sqrt(K) / s).astype(np.float32),
        "tab": np.random.uniform(0.4, 1.4, (H, J)).astype(np.float32),
        "gn": (np.random.uniform(0.5, 1.5, (H, 1)) * u[:, None]).astype(np.float32),
        "w2": (n((H, N)) / np.sqrt(H) / u[:, None]).astype(np.float32),
        "gm": (np.random.uniform(0.5, 1.5, (H, 1)) * u[:, None]).astype(np.float32),
        "w3": (n((H, N)) / np.sqrt(H) / u[:, None]).astype(np.float32),
        "offs": striped(np.random.permutation(T)[:S]),
        "n1": striped(np.random.randint(0, J, S)),
        "n2": striped(np.random.permutation(S)),
        "n3": striped(perm[:W]),
        "n4": striped(perm[W:]),
        "n5": striped(np.random.permutation(S)[:W]),
        "n6": striped(np.random.permutation(S)[:W]),
    }


def reference(x_words, x_scales, w1, tab, gn, w2, gm, w3, offs, n1, n2, n3, n4, n5, n6):
    xq = unpack_weight(x_words, x_scales)[:, unstriped(offs)]
    y = mxq(f64(w1), 0, "e4m3").T @ xq
    pa = y[:, unstriped(n3)]
    pb = y[:, unstriped(n4)]
    rb = np.maximum(0.5 * pa, pb)
    ra = pb - pa
    ds = np.zeros((H, S))
    ds[:, unstriped(n3)] = ra
    dt = ds.copy()
    dt[:, unstriped(n4)] = rb
    z2 = f64(gm) * dt
    b = mxq(f64(w3), 0, "e4m3").T @ mxq(z2, 0, "e4m3")
    z = f64(gn) * (y * f64(tab)[:, unstriped(n1)] - (0.5 * y[:, unstriped(n2)]))
    a = mxq(f64(w2), 0, "e4m3").T @ mxq(z, 0, "e4m3")
    ra2 = b[:, unstriped(n6)] - (0.5 * a[:, unstriped(n5)])
    out = a.copy()
    out[:, unstriped(n5)] = ra2
    return out

@@ -1,0 +1,203 @@
+from contextlib import ExitStack
+
+import concourse.mybir as mybir
+
+K, T, S, N, H, J, W = 512, 2048, 256, 512, 512, 512, 128
+FLOPS = 2 * S * (K * H + 2 * H * N)
+
+F32 = mybir.dt.float32
+BF16 = mybir.dt.bfloat16
+I32 = mybir.dt.int32
+U32 = mybir.dt.uint32
+U16 = mybir.dt.uint16
+U8 = mybir.dt.uint8
+FP8X4 = mybir.dt.float8_e4m3fn_x4
+ALU = mybir.AluOpType
+COPY = mybir.ActivationFunctionType.Copy
+
+P = 128
+PACK = 4
+SPARE = 16
+
+
+def tile_picked_forkputbkindglift_none_p_kernel(
+    tc, x_words, x_scales, w1, tab, gn, w2, gm, w3, offs, n1, n2, n3, n4, n5, n6, out
+):
+    nc = tc.nc
+    with ExitStack() as ctx:
+        keep = ctx.enter_context(tc.tile_pool(name="keep", bufs=1))
+        psum = ctx.enter_context(tc.psum_pool(name="psum", bufs=8))
+
+        def load_list(name, source):
+            tile = keep.tile(list(source.shape), U16, name=name)
+            nc.sync.dma_start(tile[:], source)
+            return tile
+
+        def load_weight(name, source):
+            raw = keep.tile([P, PACK, source.shape[1]], F32, name=name)
+            nc.sync.dma_start(raw[:], source.rearrange("(p j) c -> p j c", j=PACK))
+            return raw
+
+        def quantise(name, grouped):
+            width = grouped.shape[1] // PACK
+            codes = keep.tile([P, width], U32, name=name + "_codes", align_bytes=64)
+            scales = keep.tile([P, width], U8, name=name + "_scales", align_bytes=64)
+            nc.vector.quantize_mx(out=codes[:].bitcast(FP8X4), scales=scales[:], in_=grouped[:])
+            return codes, scales
+
+        def product(name, stationary, block, moving):
+            acc = psum.tile([P, S], F32, name=name, tag="acc")
+            cols = slice(P * block, P * (block + 1))
+            nc.tensor.matmul_mx(
+                out=acc[:],
+                lhsT=stationary[0][:, cols].bitcast(FP8X4),
+                lhsT_scale=stationary[1][:, cols],
+                rhs=moving[0][:].bitcast(FP8X4),
+                rhs_scale=moving[1][:],
+                start=True,
+                stop=True,
+            )
+            return acc
+
+        def group_weight(name, raw):
+            grouped = keep.tile([P, N * PACK], BF16, name=name, tag="staging", align_bytes=64)
+            nc.vector.tensor_copy(
+                out=grouped[:].rearrange("p (c i j) -> p c j i", i=4, j=PACK),
+                in_=raw[:].rearrange("p j (c i) -> p c j i", i=4),
+            )
+            return grouped
+
+        x_scale_table = keep.tile([P, T], U8, name="x_scale_table")
+        nc.gpsimd.memset(x_scale_table[:].bitcast(I32), 0)
+        offs_t = load_list("offs_t", offs)
+        w1_raw = load_weight("w1_raw", w1)
+        for q in range(4):
+            nc.sync.dma_start(
+                x_scale_table[32 * q : 32 * q + 4, :].bitcast(I32),
+                x_scales[0, 4 * q : 4 * q + 4, :].bitcast(I32),
+            )
+        x_word_table = keep.tile([P, T], U32, name="x_word_table")
+        nc.sync.dma_start(
+            x_word_table[:].bitcast(I32), x_words[0].rearrange("p n r -> p (n r)").bitcast(I32)
+        )
+        n3_t = load_list("n3_t", n3)
+        n4_t = load_list("n4_t", n4)
+        n2_t = load_list("n2_t", n2)
+        n1_t = load_list("n1_t", n1)
+        tab_rows = tab.rearrange("(p t) c -> p t c", t=PACK)
+        tab_t = [keep.tile([P, J], F32, name=f"tab{t}", tag=f"tab{t}") for t in range(PACK)]
+        for t in range(PACK):
+            nc.sync.dma_start(tab_t[t][:], tab_rows[:, t, :])
+        gn_t = keep.tile([P, PACK], F32, name="gn_t")
+        nc.sync.dma_start(gn_t[:], gn.rearrange("(p t) o -> p (t o)", t=PACK))
+        w2_raw = load_weight("w2_raw", w2)
+        w3_raw = load_weight("w3_raw", w3)
+        gm_t = keep.tile([P, PACK], F32, name="gm_t")
+        nc.sync.dma_start(gm_t[:], gm.rearrange("(p t) o -> p (t o)", t=PACK))
+        n5_t = load_list("n5_t", n5)
+        n6_t = load_list("n6_t", n6)
+
+        y = [keep.tile([P, S + SPARE], F32, name=f"y{t}", tag=f"y{t}") for t in range(PACK)]
+        for t in range(PACK):
+            nc.gpsimd.memset(y[t][:, S:], 0.0)
+
+        w1_dealt = w1_raw[:].rearrange("p j (m t) -> p m j t", t=PACK)
+        w1_grouped = [
+            keep.tile([P, 2 * P * PACK], BF16, name=f"w1_grouped{h}", align_bytes=64) for h in range(2)
+        ]
+        w1_slots = [g[:].rearrange("p (t m j) -> p m j t", t=2, j=PACK) for g in w1_grouped]
+        nc.vector.tensor_copy(w1_slots[0], w1_dealt[:, :, :, 0:2])
+        nc.scalar.activation(w1_slots[1], w1_dealt[:, :, :, 2:4], COPY)
+        x_scales_picked = keep.tile([P, S], U8, name="x_scales_picked", align_bytes=64)
+        nc.vector.tensor_copy(x_scales_picked[:], x_scale_table[:].indirect(offs_t[:]))
+        w1_q = [quantise("w1_0", w1_grouped[0])]
+        x_words_picked = keep.tile([P, S], U32, name="x_words_picked", align_bytes=64)
+        nc.vector.tensor_copy(x_words_picked[:], x_word_table[:].indirect(offs_t[:]))
+        w1_q.append(quantise("w1_1", w1_grouped[1]))
+        x_q = (x_words_picked, x_scales_picked)
+
+        for t in range(PACK):
+            acc = product(f"y_acc{t}", w1_q[t // 2], t % 2, x_q)
+            if t == 0:
+                nc.scalar.activation(y[t][:, :S], acc[:], COPY)
+            else:
+                nc.vector.tensor_copy(y[t][:, :S], acc[:])
+
+        pa = [keep.tile([P, 2, W], F32, name=f"pa{h}") for h in range(2)]
+        pb = [keep.tile([P, 2, W], F32, name=f"pb{h}") for h in range(2)]
+        lifted = []
+        dt = []
+        y_n2 = keep.tile([P, PACK, S], F32, name="y_n2")
+        y_tab = keep.tile([P, PACK, S], F32, name="y_tab")
+        diff = keep.tile([P, PACK, S], F32, name="diff", tag="diff")
+        z_grouped = keep.tile([P, S * PACK], BF16, name="z_grouped", align_bytes=64)
+
+        def put_ra(t):
+            nc.scalar.activation(dt[t][:].indirect(n3_t[:]), lifted[t // 2][:, 0, t % 2, :], COPY)
+
+        def put_rb(t):
+            nc.scalar.activation(dt[t][:].indirect(n4_t[:]), lifted[t // 2][:, 1, t % 2, :], COPY)
+
+        def z2_plane(t, z2_planes):
+            nc.vector.tensor_scalar(z2_planes[:, t, :], dt[t][:], gm_t[:, t : t + 1], None, ALU.mult)
+
+        def fetch_pairs(h):
+            for t in (2 * h, 2 * h + 1):
+                nc.scalar.activation(pa[h][:, t % 2, :], y[t][:].indirect(n3_t[:]), COPY)
+                nc.scalar.activation(pb[h][:, t % 2, :], y[t][:].indirect(n4_t[:]), COPY)
+
+        def lift(h, tag):
+            pair = keep.tile([P, 2, 2, W], F32, name=f"lifted{h}", tag=tag)
+            nc.vector.tensor_tensor(pair[:, 0], pb[h][:], pa[h][:], ALU.subtract)
+            nc.vector.scalar_tensor_tensor(pair[:, 1], pa[h][:], 0.5, pb[h][:], ALU.mult, ALU.max)
+            lifted.append(pair)
+
+        fetch_pairs(0)
+        for t in range(PACK):
+            nc.scalar.activation(y_n2[:, t, :], y[t][:].indirect(n2_t[:]), COPY)
+        fetch_pairs(1)
+        for t in range(PACK):
+            nc.vector.tensor_tensor(y_tab[:, t, :], tab_t[t][:].indirect(n1_t[:]), y[t][:, :S], ALU.mult)
+        lift(0, "tab3")
+        nc.vector.scalar_tensor_tensor(diff[:], y_n2[:], -0.5, y_tab[:], ALU.mult, ALU.add)
+        nc.vector.tensor_tensor(
+            z_grouped[:].rearrange("p (c i t) -> p c t i", i=4, t=PACK),
+            diff[:].rearrange("p t (c i) -> p c t i", i=4),
+            gn_t[:].rearrange("p (c t i) -> p c t i", c=1, i=1).to_broadcast([P, S // 4, PACK, 4]),
+            ALU.mult,
+        )
+        lift(1, "diff")
+        w2_q = quantise("w2", group_weight("w2_grouped", w2_raw))
+        z_q = quantise("z", z_grouped)
+        for t in range(PACK):
+            dt.append(keep.tile([P, S], F32, name=f"dt{t}", tag=f"y{PACK - 1 - t}"))
+        for t in range(0, PACK, 2):
+            put_ra(t)
+            put_ra(t + 1)
+            put_rb(t)
+            put_rb(t + 1)
+        w3_q = quantise("w3", group_weight("w3_grouped", w3_raw))
+        z2_grouped = keep.tile([P, S * PACK], BF16, name="z2_grouped", tag="staging", align_bytes=64)
+        for t in range(PACK):
+            z2_plane(t, z2_grouped[:].rearrange("p (c t) -> p t c", t=PACK))
+        z2_q = quantise("z2", z2_grouped)
+
+        a = [keep.tile([P, S], F32, name=f"a{m}") for m in range(N // P)]
+        b = [keep.tile([P, S], F32, name=f"b{m}") for m in range(N // P)]
+        a_n5 = [keep.tile([P, W], F32, name=f"a_n5{m}") for m in range(N // P)]
+        b_n6 = [keep.tile([P, W], F32, name=f"b_n6{m}") for m in range(N // P)]
+        ra2 = [keep.tile([P, W], F32, name=f"ra2{m}") for m in range(N // P)]
+        for m in range(N // P):
+            acc = product(f"a_acc{m}", w2_q, m, z_q)
+            nc.scalar.activation(a[m][:], acc[:], COPY)
+        for m in range(N // P):
+            nc.scalar.activation(a_n5[m][:], a[m][:].indirect(n5_t[:]), COPY)
+        for m in range(N // P):
+            acc = product(f"b_acc{m}", w3_q, m, z2_q)
+            nc.vector.tensor_copy(b[m][:], acc[:])
+        for m in range(N // P):
+            nc.scalar.activation(b_n6[m][:], b[m][:].indirect(n6_t[:]), COPY)
+            nc.vector.scalar_tensor_tensor(ra2[m][:], a_n5[m][:], -0.5, b_n6[m][:], ALU.mult, ALU.add)
+        for m in range(N // P):
+            nc.scalar.activation(a[m][:].indirect(n5_t[:]), ra2[m][:], COPY)
+            nc.sync.dma_start(out[P * m : P * (m + 1), :], a[m][:])

@@ -169,6 +169,10 @@ def tile_picked_forkputbkindglift_none_p_kernel(
         lift(1, "diff")
         w2_q = quantise("w2", group_weight("w2_grouped", w2_raw))
         z_q = quantise("z", z_grouped)
+        a = [keep.tile([P, S], F32, name=f"a{m}") for m in range(N // P)]
+        a_acc = [product(f"a_acc{m}", w2_q, m, z_q) for m in range(N // P)]
+        for m in range(2):
+            nc.vector.tensor_copy(a[m][:], a_acc[m][:])
         for t in range(PACK):
             dt.append(keep.tile([P, S], F32, name=f"dt{t}", tag=f"y{PACK - 1 - t}"))
         for t in range(0, PACK, 2):
@@ -182,14 +186,12 @@ def tile_picked_forkputbkindglift_none_p_kernel(
             z2_plane(t, z2_grouped[:].rearrange("p (c t) -> p t c", t=PACK))
         z2_q = quantise("z2", z2_grouped)
 
-        a = [keep.tile([P, S], F32, name=f"a{m}") for m in range(N // P)]
         b = [keep.tile([P, S], F32, name=f"b{m}") for m in range(N // P)]
         a_n5 = [keep.tile([P, W], F32, name=f"a_n5{m}") for m in range(N // P)]
         b_n6 = [keep.tile([P, W], F32, name=f"b_n6{m}") for m in range(N // P)]
         ra2 = [keep.tile([P, W], F32, name=f"ra2{m}") for m in range(N // P)]
-        for m in range(N // P):
-            acc = product(f"a_acc{m}", w2_q, m, z_q)
-            nc.scalar.activation(a[m][:], acc[:], COPY)
+        for m in range(2, N // P):
+            nc.scalar.activation(a[m][:], a_acc[m][:], COPY)
         for m in range(N // P):
             nc.scalar.activation(a_n5[m][:], a[m][:].indirect(n5_t[:]), COPY)
         for m in range(N // P):

@@ -45,25 +45,33 @@ def tile_picked_forkputbkindglift_none_p_kernel(
             nc.vector.quantize_mx(out=codes[:].bitcast(FP8X4), scales=scales[:], in_=grouped[:])
             return codes, scales
 
-        def product(name, stationary, block, moving):
-            acc = psum.tile([P, S], F32, name=name, tag="acc")
-            cols = slice(P * block, P * (block + 1))
+        def product(name, stationary, block, moving, cols=slice(0, S)):
+            acc = psum.tile([P, cols.stop - cols.start], F32, name=name, tag="acc")
+            rows = slice(P * block, P * (block + 1))
             nc.tensor.matmul_mx(
                 out=acc[:],
-                lhsT=stationary[0][:, cols].bitcast(FP8X4),
-                lhsT_scale=stationary[1][:, cols],
-                rhs=moving[0][:].bitcast(FP8X4),
-                rhs_scale=moving[1][:],
+                lhsT=stationary[0][:, rows].bitcast(FP8X4),
+                lhsT_scale=stationary[1][:, rows],
+                rhs=moving[0][:, cols].bitcast(FP8X4),
+                rhs_scale=moving[1][:, cols],
                 start=True,
                 stop=True,
             )
             return acc
 
+        halves = [slice(0, S // 2), slice(S // 2, S)]
+
+        def product_in_halves(name, stationary, moving, target):
+            first = product(name + "_0", stationary, 0, moving, halves[0])
+            second = product(name + "_1", stationary, 0, moving, halves[1])
+            nc.scalar.activation(target[:, halves[0]], first[:], COPY)
+            nc.vector.tensor_copy(target[:, halves[1]], second[:])
+
         def group_weight(name, raw):
-            grouped = keep.tile([P, N * PACK], BF16, name=name, tag="staging", align_bytes=64)
+            grouped = keep.tile([P, raw.shape[2] * PACK], BF16, name=name, tag="staging", align_bytes=64)
             nc.vector.tensor_copy(
                 out=grouped[:].rearrange("p (c i j) -> p c j i", i=4, j=PACK),
-                in_=raw[:].rearrange("p j (c i) -> p c j i", i=4),
+                in_=raw.rearrange("p j (c i) -> p c j i", i=4),
             )
             return grouped
 
@@ -76,21 +84,22 @@ def tile_picked_forkputbkindglift_none_p_kernel(
                 x_scale_table[32 * q : 32 * q + 4, :].bitcast(I32),
                 x_scales[0, 4 * q : 4 * q + 4, :].bitcast(I32),
             )
+        n2_t = load_list("n2_t", n2)
         x_word_table = keep.tile([P, T], U32, name="x_word_table")
         nc.sync.dma_start(
             x_word_table[:].bitcast(I32), x_words[0].rearrange("p n r -> p (n r)").bitcast(I32)
         )
-        n3_t = load_list("n3_t", n3)
-        n4_t = load_list("n4_t", n4)
-        n2_t = load_list("n2_t", n2)
         n1_t = load_list("n1_t", n1)
         tab_rows = tab.rearrange("(p t) c -> p t c", t=PACK)
-        tab_t = [keep.tile([P, J], F32, name=f"tab{t}", tag=f"tab{t}") for t in range(PACK)]
-        for t in range(PACK):
+        tab_t = [keep.tile([P, J], F32, name=f"tab{t}") for t in range(PACK)]
+        nc.sync.dma_start(tab_t[0][:], tab_rows[:, 0, :])
+        n3_t = load_list("n3_t", n3)
+        n4_t = load_list("n4_t", n4)
+        for t in range(1, PACK):
             nc.sync.dma_start(tab_t[t][:], tab_rows[:, t, :])
+        w2_raw = load_weight("w2_raw", w2)
         gn_t = keep.tile([P, PACK], F32, name="gn_t")
         nc.sync.dma_start(gn_t[:], gn.rearrange("(p t) o -> p (t o)", t=PACK))
-        w2_raw = load_weight("w2_raw", w2)
         w3_raw = load_weight("w3_raw", w3)
         gm_t = keep.tile([P, PACK], F32, name="gm_t")
         nc.sync.dma_start(gm_t[:], gm.rearrange("(p t) o -> p (t o)", t=PACK))
@@ -116,19 +125,17 @@ def tile_picked_forkputbkindglift_none_p_kernel(
         w1_q.append(quantise("w1_1", w1_grouped[1]))
         x_q = (x_words_picked, x_scales_picked)
 
-        for t in range(PACK):
+        product_in_halves("y_acc0", w1_q[0], x_q, y[0])
+        for t in range(1, PACK):
             acc = product(f"y_acc{t}", w1_q[t // 2], t % 2, x_q)
-            if t == 0:
-                nc.scalar.activation(y[t][:, :S], acc[:], COPY)
-            else:
-                nc.vector.tensor_copy(y[t][:, :S], acc[:])
+            nc.vector.tensor_copy(y[t][:, :S], acc[:])
 
         pa = [keep.tile([P, 2, W], F32, name=f"pa{h}") for h in range(2)]
         pb = [keep.tile([P, 2, W], F32, name=f"pb{h}") for h in range(2)]
         lifted = []
         dt = []
         y_n2 = keep.tile([P, PACK, S], F32, name="y_n2")
-        y_tab = keep.tile([P, PACK, S], F32, name="y_tab")
+        y_tab = keep.tile([P, PACK, S], F32, name="y_tab", tag="y_tab")
         diff = keep.tile([P, PACK, S], F32, name="diff", tag="diff")
         z_grouped = keep.tile([P, S * PACK], BF16, name="z_grouped", align_bytes=64)
 
@@ -138,8 +145,8 @@ def tile_picked_forkputbkindglift_none_p_kernel(
         def put_rb(t):
             nc.scalar.activation(dt[t][:].indirect(n4_t[:]), lifted[t // 2][:, 1, t % 2, :], COPY)
 
-        def z2_plane(t, z2_planes):
-            nc.vector.tensor_scalar(z2_planes[:, t, :], dt[t][:], gm_t[:, t : t + 1], None, ALU.mult)
+        def z2_plane(t, z2_planes, cols):
+            nc.vector.tensor_scalar(z2_planes[:, t, cols], dt[t][:, cols], gm_t[:, t : t + 1], None, ALU.mult)
 
         def fetch_pairs(h):
             for t in (2 * h, 2 * h + 1):
@@ -152,14 +159,14 @@ def tile_picked_forkputbkindglift_none_p_kernel(
             nc.vector.scalar_tensor_tensor(pair[:, 1], pa[h][:], 0.5, pb[h][:], ALU.mult, ALU.max)
             lifted.append(pair)
 
-        fetch_pairs(0)
         for t in range(PACK):
             nc.scalar.activation(y_n2[:, t, :], y[t][:].indirect(n2_t[:]), COPY)
+        fetch_pairs(0)
         fetch_pairs(1)
         for t in range(PACK):
             nc.vector.tensor_tensor(y_tab[:, t, :], tab_t[t][:].indirect(n1_t[:]), y[t][:, :S], ALU.mult)
-        lift(0, "tab3")
         nc.vector.scalar_tensor_tensor(diff[:], y_n2[:], -0.5, y_tab[:], ALU.mult, ALU.add)
+        lift(0, "y_tab")
         nc.vector.tensor_tensor(
             z_grouped[:].rearrange("p (c i t) -> p c t i", i=4, t=PACK),
             diff[:].rearrange("p t (c i) -> p c t i", i=4),
@@ -167,7 +174,7 @@ def tile_picked_forkputbkindglift_none_p_kernel(
             ALU.mult,
         )
         lift(1, "diff")
-        w2_q = quantise("w2", group_weight("w2_grouped", w2_raw))
+        w2_q = quantise("w2", group_weight("w2_grouped", w2_raw[:]))
         z_q = quantise("z", z_grouped)
         a = [keep.tile([P, S], F32, name=f"a{m}") for m in range(N // P)]
         a_acc = [product(f"a_acc{m}", w2_q, m, z_q) for m in range(N // P)]
@@ -180,26 +187,52 @@ def tile_picked_forkputbkindglift_none_p_kernel(
             put_ra(t + 1)
             put_rb(t)
             put_rb(t + 1)
-        w3_q = quantise("w3", group_weight("w3_grouped", w3_raw))
+        w3_q = [quantise("w3_0", group_weight("w3_grouped0", w3_raw[:, :, : 3 * P]))]
         z2_grouped = keep.tile([P, S * PACK], BF16, name="z2_grouped", tag="staging", align_bytes=64)
-        for t in range(PACK):
-            z2_plane(t, z2_grouped[:].rearrange("p (c t) -> p t c", t=PACK))
-        z2_q = quantise("z2", z2_grouped)
+        z2_planes = z2_grouped[:].rearrange("p (c t) -> p t c", t=PACK)
+        for t in range(PACK - 1):
+            z2_plane(t, z2_planes, slice(0, S))
+        for cols in halves:
+            z2_plane(PACK - 1, z2_planes, cols)
+        z2_codes = keep.tile([P, S], U32, name="z2_codes", align_bytes=64)
+        z2_scales = keep.tile([P, S], U8, name="z2_scales", align_bytes=64)
+        for cols in halves:
+            nc.vector.quantize_mx(
+                out=z2_codes[:, cols].bitcast(FP8X4),
+                scales=z2_scales[:, cols],
+                in_=z2_grouped[:, PACK * cols.start : PACK * cols.stop],
+            )
+        z2_q = (z2_codes, z2_scales)
+        w3_last = group_weight("w3_grouped1", w3_raw[:, :, 3 * P :])
 
-        b = [keep.tile([P, S], F32, name=f"b{m}") for m in range(N // P)]
+        b = [keep.tile([P, S], F32, name=f"b{m}", tag=f"b{m}") for m in range(N // P)]
         a_n5 = [keep.tile([P, W], F32, name=f"a_n5{m}") for m in range(N // P)]
         b_n6 = [keep.tile([P, W], F32, name=f"b_n6{m}") for m in range(N // P)]
-        ra2 = [keep.tile([P, W], F32, name=f"ra2{m}") for m in range(N // P)]
         for m in range(2, N // P):
             nc.scalar.activation(a[m][:], a_acc[m][:], COPY)
         for m in range(N // P):
             nc.scalar.activation(a_n5[m][:], a[m][:].indirect(n5_t[:]), COPY)
-        for m in range(N // P):
-            acc = product(f"b_acc{m}", w3_q, m, z2_q)
-            nc.vector.tensor_copy(b[m][:], acc[:])
-        for m in range(N // P):
+
+        def fetch_b(m):
             nc.scalar.activation(b_n6[m][:], b[m][:].indirect(n6_t[:]), COPY)
-            nc.vector.scalar_tensor_tensor(ra2[m][:], a_n5[m][:], -0.5, b_n6[m][:], ALU.mult, ALU.add)
-        for m in range(N // P):
-            nc.scalar.activation(a[m][:].indirect(n5_t[:]), ra2[m][:], COPY)
+
+        def make_b(m, weights, block):
+            acc = product(f"b_acc{m}", weights, block, z2_q)
+            nc.vector.tensor_copy(b[m][:], acc[:])
+            fetch_b(m)
+
+        def join(m, tag):
+            ra2 = keep.tile([P, W], F32, name=f"ra2_{m}", tag=tag)
+            nc.vector.scalar_tensor_tensor(ra2[:], a_n5[m][:], -0.5, b_n6[m][:], ALU.mult, ALU.add)
+            nc.scalar.activation(a[m][:].indirect(n5_t[:]), ra2[:], COPY)
             nc.sync.dma_start(out[P * m : P * (m + 1), :], a[m][:])
+
+        product_in_halves("b_acc0", w3_q[0], z2_q, b[0])
+        fetch_b(0)
+        make_b(1, w3_q[0], 1)
+        join(0, "b0")
+        make_b(2, w3_q[0], 2)
+        make_b(3, quantise("w3_1", w3_last), 0)
+        join(1, "b2")
+        join(2, "b1")
+        join(3, "b3")

@@ -178,7 +178,7 @@ def tile_picked_forkputbkindglift_none_p_kernel(
         z_q = quantise("z", z_grouped)
         a = [keep.tile([P, S], F32, name=f"a{m}") for m in range(N // P)]
         a_acc = [product(f"a_acc{m}", w2_q, m, z_q) for m in range(N // P)]
-        for m in range(2):
+        for m in range(1):
             nc.vector.tensor_copy(a[m][:], a_acc[m][:])
         for t in range(PACK):
             dt.append(keep.tile([P, S], F32, name=f"dt{t}", tag=f"y{PACK - 1 - t}"))
@@ -208,7 +208,7 @@ def tile_picked_forkputbkindglift_none_p_kernel(
         b = [keep.tile([P, S], F32, name=f"b{m}", tag=f"b{m}") for m in range(N // P)]
         a_n5 = [keep.tile([P, W], F32, name=f"a_n5{m}") for m in range(N // P)]
         b_n6 = [keep.tile([P, W], F32, name=f"b_n6{m}") for m in range(N // P)]
-        for m in range(2, N // P):
+        for m in range(1, N // P):
             nc.scalar.activation(a[m][:], a_acc[m][:], COPY)
         for m in range(N // P):
             nc.scalar.activation(a_n5[m][:], a[m][:].indirect(n5_t[:]), COPY)

from contextlib import ExitStack

import concourse.mybir as mybir

K, T, S, N, H, J, W = 512, 2048, 256, 512, 512, 512, 128
FLOPS = 2 * S * (K * H + 2 * H * N)

F32 = mybir.dt.float32
BF16 = mybir.dt.bfloat16
I32 = mybir.dt.int32
U32 = mybir.dt.uint32
U16 = mybir.dt.uint16
U8 = mybir.dt.uint8
FP8X4 = mybir.dt.float8_e4m3fn_x4
ALU = mybir.AluOpType
COPY = mybir.ActivationFunctionType.Copy

P = 128
PACK = 4
SPARE = 16


def tile_picked_forkputbkindglift_none_p_kernel(
    tc, x_words, x_scales, w1, tab, gn, w2, gm, w3, offs, n1, n2, n3, n4, n5, n6, out
):
    nc = tc.nc
    with ExitStack() as ctx:
        keep = ctx.enter_context(tc.tile_pool(name="keep", bufs=1))
        psum = ctx.enter_context(tc.psum_pool(name="psum", bufs=8))

        def load_list(name, source):
            tile = keep.tile(list(source.shape), U16, name=name)
            nc.sync.dma_start(tile[:], source)
            return tile

        def load_weight(name, source):
            raw = keep.tile([P, PACK, source.shape[1]], F32, name=name)
            nc.sync.dma_start(raw[:], source.rearrange("(p j) c -> p j c", j=PACK))
            return raw

        def quantise(name, grouped):
            width = grouped.shape[1] // PACK
            codes = keep.tile([P, width], U32, name=name + "_codes", align_bytes=64)
            scales = keep.tile([P, width], U8, name=name + "_scales", align_bytes=64)
            nc.vector.quantize_mx(out=codes[:].bitcast(FP8X4), scales=scales[:], in_=grouped[:])
            return codes, scales

        def product(name, stationary, block, moving, cols=slice(0, S)):
            acc = psum.tile([P, cols.stop - cols.start], F32, name=name, tag="acc")
            rows = slice(P * block, P * (block + 1))
            nc.tensor.matmul_mx(
                out=acc[:],
                lhsT=stationary[0][:, rows].bitcast(FP8X4),
                lhsT_scale=stationary[1][:, rows],
                rhs=moving[0][:, cols].bitcast(FP8X4),
                rhs_scale=moving[1][:, cols],
                start=True,
                stop=True,
            )
            return acc

        halves = [slice(0, S // 2), slice(S // 2, S)]

        def product_in_halves(name, stationary, moving, target):
            first = product(name + "_0", stationary, 0, moving, halves[0])
            second = product(name + "_1", stationary, 0, moving, halves[1])
            nc.scalar.activation(target[:, halves[0]], first[:], COPY)
            nc.vector.tensor_copy(target[:, halves[1]], second[:])

        def group_weight(name, raw):
            grouped = keep.tile([P, raw.shape[2] * PACK], BF16, name=name, tag="staging", align_bytes=64)
            nc.vector.tensor_copy(
                out=grouped[:].rearrange("p (c i j) -> p c j i", i=4, j=PACK),
                in_=raw.rearrange("p j (c i) -> p c j i", i=4),
            )
            return grouped

        x_scale_table = keep.tile([P, T], U8, name="x_scale_table")
        nc.gpsimd.memset(x_scale_table[:].bitcast(I32), 0)
        offs_t = load_list("offs_t", offs)
        w1_raw = load_weight("w1_raw", w1)
        for q in range(4):
            nc.sync.dma_start(
                x_scale_table[32 * q : 32 * q + 4, :].bitcast(I32),
                x_scales[0, 4 * q : 4 * q + 4, :].bitcast(I32),
            )
        n2_t = load_list("n2_t", n2)
        x_word_table = keep.tile([P, T], U32, name="x_word_table")
        nc.sync.dma_start(
            x_word_table[:].bitcast(I32), x_words[0].rearrange("p n r -> p (n r)").bitcast(I32)
        )
        n1_t = load_list("n1_t", n1)
        tab_rows = tab.rearrange("(p t) c -> p t c", t=PACK)
        tab_t = [keep.tile([P, J], F32, name=f"tab{t}") for t in range(PACK)]
        nc.sync.dma_start(tab_t[0][:], tab_rows[:, 0, :])
        n3_t = load_list("n3_t", n3)
        n4_t = load_list("n4_t", n4)
        for t in range(1, PACK):
            nc.sync.dma_start(tab_t[t][:], tab_rows[:, t, :])
        w2_raw = load_weight("w2_raw", w2)
        gn_t = keep.tile([P, PACK], F32, name="gn_t")
        nc.sync.dma_start(gn_t[:], gn.rearrange("(p t) o -> p (t o)", t=PACK))
        w3_raw = load_weight("w3_raw", w3)
        gm_t = keep.tile([P, PACK], F32, name="gm_t")
        nc.sync.dma_start(gm_t[:], gm.rearrange("(p t) o -> p (t o)", t=PACK))
        n5_t = load_list("n5_t", n5)
        n6_t = load_list("n6_t", n6)

        y = [keep.tile([P, S + SPARE], F32, name=f"y{t}", tag=f"y{t}") for t in range(PACK)]
        for t in range(PACK):
            nc.gpsimd.memset(y[t][:, S:], 0.0)

        w1_dealt = w1_raw[:].rearrange("p j (m t) -> p m j t", t=PACK)
        w1_grouped = [
            keep.tile([P, 2 * P * PACK], BF16, name=f"w1_grouped{h}", align_bytes=64) for h in range(2)
        ]
        w1_slots = [g[:].rearrange("p (t m j) -> p m j t", t=2, j=PACK) for g in w1_grouped]
        nc.vector.tensor_copy(w1_slots[0], w1_dealt[:, :, :, 0:2])
        nc.scalar.activation(w1_slots[1], w1_dealt[:, :, :, 2:4], COPY)
        x_scales_picked = keep.tile([P, S], U8, name="x_scales_picked", align_bytes=64)
        nc.vector.tensor_copy(x_scales_picked[:], x_scale_table[:].indirect(offs_t[:]))
        w1_q = [quantise("w1_0", w1_grouped[0])]
        x_words_picked = keep.tile([P, S], U32, name="x_words_picked", align_bytes=64)
        nc.vector.tensor_copy(x_words_picked[:], x_word_table[:].indirect(offs_t[:]))
        w1_q.append(quantise("w1_1", w1_grouped[1]))
        x_q = (x_words_picked, x_scales_picked)

        product_in_halves("y_acc0", w1_q[0], x_q, y[0])
        for t in range(1, PACK):
            acc = product(f"y_acc{t}", w1_q[t // 2], t % 2, x_q)
            nc.vector.tensor_copy(y[t][:, :S], acc[:])

        pa = [keep.tile([P, 2, W], F32, name=f"pa{h}") for h in range(2)]
        pb = [keep.tile([P, 2, W], F32, name=f"pb{h}") for h in range(2)]
        lifted = []
        dt = []
        y_n2 = keep.tile([P, PACK, S], F32, name="y_n2")
        y_tab = keep.tile([P, PACK, S], F32, name="y_tab", tag="y_tab")
        diff = keep.tile([P, PACK, S], F32, name="diff", tag="diff")
        z_grouped = keep.tile([P, S * PACK], BF16, name="z_grouped", align_bytes=64)

        def put_ra(t):
            nc.scalar.activation(dt[t][:].indirect(n3_t[:]), lifted[t // 2][:, 0, t % 2, :], COPY)

        def put_rb(t):
            nc.scalar.activation(dt[t][:].indirect(n4_t[:]), lifted[t // 2][:, 1, t % 2, :], COPY)

        def z2_plane(t, z2_planes, cols):
            nc.vector.tensor_scalar(z2_planes[:, t, cols], dt[t][:, cols], gm_t[:, t : t + 1], None, ALU.mult)

        def fetch_pairs(h):
            for t in (2 * h, 2 * h + 1):
                nc.scalar.activation(pa[h][:, t % 2, :], y[t][:].indirect(n3_t[:]), COPY)
                nc.scalar.activation(pb[h][:, t % 2, :], y[t][:].indirect(n4_t[:]), COPY)

        def lift(h, tag):
            pair = keep.tile([P, 2, 2, W], F32, name=f"lifted{h}", tag=tag)
            nc.vector.tensor_tensor(pair[:, 0], pb[h][:], pa[h][:], ALU.subtract)
            nc.vector.scalar_tensor_tensor(pair[:, 1], pa[h][:], 0.5, pb[h][:], ALU.mult, ALU.max)
            lifted.append(pair)

        for t in range(PACK):
            nc.scalar.activation(y_n2[:, t, :], y[t][:].indirect(n2_t[:]), COPY)
        fetch_pairs(0)
        fetch_pairs(1)
        for t in range(PACK):
            nc.vector.tensor_tensor(y_tab[:, t, :], tab_t[t][:].indirect(n1_t[:]), y[t][:, :S], ALU.mult)
        nc.vector.scalar_tensor_tensor(diff[:], y_n2[:], -0.5, y_tab[:], ALU.mult, ALU.add)
        lift(0, "y_tab")
        nc.vector.tensor_tensor(
            z_grouped[:].rearrange("p (c i t) -> p c t i", i=4, t=PACK),
            diff[:].rearrange("p t (c i) -> p c t i", i=4),
            gn_t[:].rearrange("p (c t i) -> p c t i", c=1, i=1).to_broadcast([P, S // 4, PACK, 4]),
            ALU.mult,
        )
        lift(1, "diff")
        w2_q = quantise("w2", group_weight("w2_grouped", w2_raw[:]))
        z_q = quantise("z", z_grouped)
        a = [keep.tile([P, S], F32, name=f"a{m}") for m in range(N // P)]
        a_acc = [product(f"a_acc{m}", w2_q, m, z_q) for m in range(N // P)]
        for m in range(1):
            nc.vector.tensor_copy(a[m][:], a_acc[m][:])
        for t in range(PACK):
            dt.append(keep.tile([P, S], F32, name=f"dt{t}", tag=f"y{PACK - 1 - t}"))
        for t in range(0, PACK, 2):
            put_ra(t)
            put_ra(t + 1)
            put_rb(t)
            put_rb(t + 1)
        w3_q = [quantise("w3_0", group_weight("w3_grouped0", w3_raw[:, :, : 3 * P]))]
        z2_grouped = keep.tile([P, S * PACK], BF16, name="z2_grouped", tag="staging", align_bytes=64)
        z2_planes = z2_grouped[:].rearrange("p (c t) -> p t c", t=PACK)
        for t in range(PACK - 1):
            z2_plane(t, z2_planes, slice(0, S))
        for cols in halves:
            z2_plane(PACK - 1, z2_planes, cols)
        z2_codes = keep.tile([P, S], U32, name="z2_codes", align_bytes=64)
        z2_scales = keep.tile([P, S], U8, name="z2_scales", align_bytes=64)
        for cols in halves:
            nc.vector.quantize_mx(
                out=z2_codes[:, cols].bitcast(FP8X4),
                scales=z2_scales[:, cols],
                in_=z2_grouped[:, PACK * cols.start : PACK * cols.stop],
            )
        z2_q = (z2_codes, z2_scales)
        w3_last = group_weight("w3_grouped1", w3_raw[:, :, 3 * P :])

        b = [keep.tile([P, S], F32, name=f"b{m}", tag=f"b{m}") for m in range(N // P)]
        a_n5 = [keep.tile([P, W], F32, name=f"a_n5{m}") for m in range(N // P)]
        b_n6 = [keep.tile([P, W], F32, name=f"b_n6{m}") for m in range(N // P)]
        for m in range(1, N // P):
            nc.scalar.activation(a[m][:], a_acc[m][:], COPY)
        for m in range(N // P):
            nc.scalar.activation(a_n5[m][:], a[m][:].indirect(n5_t[:]), COPY)

        def fetch_b(m):
            nc.scalar.activation(b_n6[m][:], b[m][:].indirect(n6_t[:]), COPY)

        def make_b(m, weights, block):
            acc = product(f"b_acc{m}", weights, block, z2_q)
            nc.vector.tensor_copy(b[m][:], acc[:])
            fetch_b(m)

        def join(m, tag):
            ra2 = keep.tile([P, W], F32, name=f"ra2_{m}", tag=tag)
            nc.vector.scalar_tensor_tensor(ra2[:], a_n5[m][:], -0.5, b_n6[m][:], ALU.mult, ALU.add)
            nc.scalar.activation(a[m][:].indirect(n5_t[:]), ra2[:], COPY)
            nc.sync.dma_start(out[P * m : P * (m + 1), :], a[m][:])

        product_in_halves("b_acc0", w3_q[0], z2_q, b[0])
        fetch_b(0)
        make_b(1, w3_q[0], 1)
        join(0, "b0")
        make_b(2, w3_q[0], 2)
        make_b(3, quantise("w3_1", w3_last), 0)
        join(1, "b2")
        join(2, "b1")
        join(3, "b3")
